import numpy as np
CORES = [8,136,40,168]
N = 4
J, Q = 256, 2048
def entries(a): return a.T.reshape(-1)
def pack(v, P): return np.ascontiguousarray(np.asarray(v, np.int32).reshape(-1, P).T)
def split(rng, total, parts):
    c = np.sort(rng.integers(0, total + 1, parts - 1)); return np.diff(np.concatenate([[0], c, [total]]))
def lists(rng, how):
    tot = 1 + split(rng, int(rng.integers(N * Q - Q // 2, N * Q + 1)) - N, N)
    if how == "gaps": tot = split(rng, (N - 1) * Q, N)
    if how == "short": tot = split(rng, Q * int(rng.integers(1, N - 1)) + int(rng.integers(1, Q)), N)
    L = np.stack([split(rng, int(t), J) for t in tot])
    if how == "gaps":
        L = np.zeros((N, J), np.int64)
        for r in range(N): m = 1 if r & 1 else 8; L[r, 1 + rng.permutation(J - 2)[:m]] = split(rng, int(tot[r]), m)
    if how == "lone":
        L = np.zeros((N, J), np.int64); L[int(rng.integers(N)), int(rng.integers(J))] = N * Q
    if how == "ones":
        L = np.zeros((N, J), np.int64)
        for r in range(N): L[r, rng.permutation(J)[:min(J, Q // N)]] = 1
    if how == "void": L[:] = 0
    return {"ln": np.stack([pack(l, 16) for l in L])}
def setup_inputs(rng):
    return dict({"x": rng.standard_normal((N, 128, J), dtype=np.float32)}, **lists(rng, "uniform"))
def setup_inputs_gaps(rng):
    d = setup_inputs(rng); d.update(lists(rng, "gaps"))
    for k in ("x",): d[k] = (d[k].astype(np.float32) * 1048576.0).astype(d[k].dtype)
    return d
def setup_inputs_lone(rng):
    d = setup_inputs(rng); d.update(lists(rng, "lone"))
    for k in ("x",): d[k] = (d[k].astype(np.float32) * (1 / 1024.0)).astype(d[k].dtype)
    return d
def setup_inputs_ones(rng):
    d = setup_inputs(rng); d.update(lists(rng, "ones"))
    return d
def setup_inputs_short(rng):
    d = setup_inputs(rng); d.update(lists(rng, "short"))
    return d
def setup_inputs_void(rng):
    d = setup_inputs(rng); d.update(lists(rng, "void"))
    return d
def check_inputs(x):
    bad = []
    if x["ln"].min() < 0 or x["ln"].max() >= N * Q + 1: bad.append("ln out of range")
    if int(x["ln"].sum()) > N * Q: bad.append("the lengths come to more than N * Q")
    return bad
def reference(x, ln):
    got = np.concatenate([np.repeat(x[r], entries(ln[r]), axis=1) for r in range(N)], axis=1)[:, :N * Q]
    Y = np.zeros((128, N * Q), x.dtype); Y[:, :got.shape[1]] = got
    return {"y": np.stack([Y[:, Q * r:Q * r + Q] for r in range(N)])}

@@ -1,0 +1,195 @@
+from concourse.bass import DstId, RemoteDMATransfer
+from concourse.mybir import dt, AluOpType, ActivationFunctionType
+
+R, J, Q, P = 4, 256, 2048, 128
+NJ = R * J
+K = NJ // P
+C = Q // 16
+SW = 144
+PIECES = [("v", 0, 384), ("s", 384, 768), ("v", 768, 1408), ("s", 1408, 2048)]
+
+SCRATCH = {
+    "win": ("sbuf", [P, NJ + 4], "float32"),
+    "ysb": ("sbuf", [P, Q], "float32"),
+    "lall": ("dram", [R * P, J // P], "int32"),
+    "lsb": ("sbuf", [P, K], "int32"),
+    "lf": ("sbuf", [P, K], "float32"),
+    "ones": ("sbuf", [P, K], "float32"),
+    "scan": ("sbuf", [P, K + 4], "float32"),
+    "colk": ("sbuf", [P, P], "int32"),
+    "ck2": ("sbuf", [P, P], "int32"),
+    "rowp": ("sbuf", [P, 4], "int32"),
+    "t5": ("sbuf", [P, 4], "int32"),
+    "t1": ("sbuf", [P, 4], "int32"),
+    "th": ("sbuf", [P, 4], "int32"),
+    "tu": ("sbuf", [P, 4], "int32"),
+    "tv": ("sbuf", [P, 4], "int32"),
+    "key2": ("sbuf", [P, 4], "float32"),
+    "keyf": ("sbuf", [P, 4], "float32"),
+    "meq": ("sbuf", [P, P], "float32"),
+    "mle": ("sbuf", [P, P], "float32"),
+    "mlt": ("sbuf", [P, P], "float32"),
+    "meqp": ("sbuf", [P, P], "float32"),
+    "meqn": ("sbuf", [P, P], "float32"),
+    "nb": ("sbuf", [P, K], "float32"),
+    "cumi": ("sbuf", [P, K], "int32"),
+    "loi": ("sbuf", [P, K], "int32"),
+    "lof": ("sbuf", [P, K], "float32"),
+    "grid": ("sbuf", [P, C + 4], "float32"),
+    "ltab": ("sbuf", [P, P], "bfloat16"),
+    "sg": ("sbuf", [P, K * SW], "bfloat16"),
+    "gt": ("sbuf", [P, K * P], "bfloat16"),
+    "le": ("sbuf", [P, K * P], "bfloat16"),
+    "offs": ("sbuf", [P, C], "uint16"),
+    "pcum": ("psum", [P, 512], "float32"),
+    "pcnt": ("psum", [P, 512], "float32"),
+}
+SEMAPHORES = ["lnl", "xl", "larr", "xarr", "lsent", "xsent", "lld", "gi", "v", "s", "t", "st"]
+
+
+def ones_in(mask):
+    return bin(mask).count("1")
+
+
+def rank_program(g, core, T, topo):
+    rank = T.rank_of(core)
+    if rank is None:
+        return
+    A = AluOpType
+    F = ActivationFunctionType
+    sem = T.sem
+    n = len(T.cores)
+    peers = [T.cores[(rank + i) % n] for i in range(1, n)]
+    wide = topo.mask(core, peers[0])
+    for d in peers:
+        wide &= topo.mask(core, d)
+    one = wide & -wide
+    dst = []
+    for d in peers:
+        rid, pnc = topo.addr(d, core)
+        dst.append(DstId(rid=rid, pnc=pnc))
+    lslot = T.lall[rank * P:(rank + 1) * P, :]
+    xslot = T.win[:, rank * J:(rank + 1) * J]
+    SALL = (n - 1)
+
+    g.sync.dma_start(lslot, T.ln[:]).then_inc(sem.lnl, 16)
+    g.scalar.dma_start(xslot, T.x[:]).then_inc(sem.xl, 16)
+
+    g.iota(T.colk[:], [[32, 4], [1, 16], [16, 2]], 0, 0).then_inc(sem.gi, 1)
+    g.iota(T.rowp[:, 0:1], [[0, 1]], 0, 1).then_inc(sem.gi, 1)
+    g.wait_ge(sem.lnl, 16)
+    g.remote_dma_fused([RemoteDMATransfer(dst_ids=dst, dma_engine_mask=one, remote_sem=sem.larr,
+                                          srcs=[lslot], dsts=[lslot] * SALL)], local_sem=sem.lsent)
+    g.wait_ge(sem.xl, 16)
+    g.remote_dma_fused([RemoteDMATransfer(dst_ids=dst, dma_engine_mask=wide, remote_sem=sem.xarr,
+                                          srcs=[xslot], dsts=[xslot] * SALL)], local_sem=sem.xsent)
+    g.iota(T.grid[:, 0:C + 1], [[32, C + 1]], 2 * rank * Q - 1, 0,
+           allow_small_or_imprecise_dtypes=True).then_inc(sem.gi, 1)
+    g.iota(T.ltab[:], [[0, P // 16], [1, 16]], 0, 0, allow_small_or_imprecise_dtypes=True).then_inc(sem.gi, 1)
+
+    g.sync.wait_ge(sem.lnl, 16)
+    g.sync.wait_ge(sem.larr, SALL * ones_in(one))
+    g.sync.dma_start(T.lsb[:], T.lall[:]).then_inc(sem.lld, 16)
+
+    vn = [0]
+    V = g.vector
+
+    def vi(ins):
+        ins.then_inc(sem.v, 1)
+        vn[0] += 1
+        return vn[0]
+
+    def vw():
+        V.wait_ge(sem.v, vn[0])
+
+    vi(V.memset(T.win[:, NJ:NJ + 4], 0.0))
+    vi(V.memset(T.scan[:, 0:1], 0.0))
+    vi(V.memset(T.ones[:], 1.0))
+    V.wait_ge(sem.gi, 2)
+    vi(V.tensor_scalar(T.ck2[:], T.colk[:], 4, None, A.arith_shift_right))
+    vi(V.tensor_scalar(T.t5[:, 0:1], T.rowp[:, 0:1], 5, None, A.arith_shift_right))
+    vi(V.tensor_scalar(T.t1[:, 0:1], T.rowp[:, 0:1], 1, None, A.bitwise_and))
+    vi(V.tensor_scalar(T.th[:, 0:1], T.rowp[:, 0:1], 1, None, A.arith_shift_right))
+    vw()
+    vi(V.tensor_tensor(T.tu[:, 0:1], T.t5[:, 0:1], T.t1[:, 0:1], A.add))
+    vw()
+    vi(V.tensor_tensor(T.key2[:, 0:1], T.tu[:, 0:1], T.t5[:, 0:1], A.add))
+    vi(V.tensor_scalar(T.tv[:, 0:1], T.tu[:, 0:1], 16.0, None, A.mult))
+    vw()
+    vi(V.tensor_tensor(T.keyf[:, 0:1], T.tv[:, 0:1], T.th[:, 0:1], A.add))
+    vi(V.tensor_scalar(T.meq[:], T.ck2[:], T.key2[:, 0:1], None, A.is_equal))
+    vi(V.tensor_scalar(T.mlt[:], T.ck2[:], T.key2[:, 0:1], None, A.is_gt))
+    vw()
+    vi(V.tensor_scalar(T.mle[:], T.colk[:], T.keyf[:, 0:1], None, A.is_ge))
+    vw()
+    vi(V.tensor_tensor(T.meqp[:], T.meq[:], T.mle[:], A.mult))
+    vw()
+    vi(V.tensor_tensor(T.meqn[:], T.meq[:], T.meqp[:], A.subtract))
+
+    V.wait_ge(sem.lld, 16)
+    vi(V.tensor_copy(T.lf[:], T.lsb[:]))
+    vw()
+    v_scan = vi(V.tensor_tensor_scan(T.scan[:, 1:K + 1], T.ones[:], T.lf[:], 0.0, A.mult, A.add))
+
+    g.tensor.wait_ge(sem.v, v_scan)
+    g.tensor.matmul(T.pcum[:, K:K + 1], T.mlt[:], T.scan[:, K:K + 1], True, True)
+    g.tensor.matmul(T.pcum[:, 0:K], T.meqp[:], T.scan[:, 1:K + 1], True, False)
+    g.tensor.matmul(T.pcum[:, 0:K], T.meqn[:], T.scan[:, 0:K], False, True).then_inc(sem.t, 1)
+
+    V.wait_ge(sem.t, 1)
+    vi(V.tensor_scalar(T.cumi[:], T.pcum[:, 0:K], T.pcum[:, K:K + 1], None, A.add))
+    v_nb = vi(V.tensor_scalar(T.nb[:], T.pcum[:, 0:K], T.pcum[:, K:K + 1], -2.0, A.add, A.mult))
+    vw()
+    vi(V.tensor_scalar(T.loi[:], T.cumi[:], 15, None, A.bitwise_and))
+    vw()
+    vi(V.tensor_copy(T.lof[:], T.loi[:]))
+    vw()
+    V.wait_ge(sem.gi, 4)
+    v_cmp = []
+    for k in range(K):
+        vi(V.tensor_scalar(T.gt[:, k * P:(k + 1) * P], T.ltab[:], T.lof[:, k:k + 1], None, A.is_lt))
+        v_cmp.append(vi(V.tensor_scalar(T.le[:, k * P:(k + 1) * P], T.ltab[:], T.lof[:, k:k + 1], None, A.is_ge)))
+
+    sn = [0]
+    S = g.scalar
+
+    def si(ins):
+        ins.then_inc(sem.s, 1)
+        sn[0] += 1
+        return sn[0]
+
+    S.wait_ge(sem.gi, 4)
+    S.wait_ge(sem.v, v_nb)
+    s_sg = []
+    for k in range(K):
+        s_sg.append(si(S.activation(T.sg[:, k * SW:k * SW + C + 1], T.grid[:, 0:C + 1], F.Sign,
+                                    bias=T.nb[:, k:k + 1])))
+
+    for k in range(K):
+        g.tensor.wait_ge(sem.v, v_cmp[k])
+        g.tensor.wait_ge(sem.s, s_sg[k])
+        g.tensor.matmul(T.pcnt[:, 0:C], T.gt[:, k * P:(k + 1) * P], T.sg[:, k * SW:k * SW + C], k == 0, False)
+        last = g.tensor.matmul(T.pcnt[:, 0:C], T.le[:, k * P:(k + 1) * P], T.sg[:, k * SW + 1:k * SW + C + 1],
+                               False, k == K - 1)
+    last.then_inc(sem.t, 1)
+
+    V.wait_ge(sem.t, 2)
+    v_off = vi(V.tensor_scalar(T.offs[:], T.pcnt[:, 0:C], 0.5, float(NJ // 2), A.mult, A.add))
+    nx = SALL * ones_in(wide)
+    for q in (V, S):
+        q.wait_ge(sem.v, v_off)
+        q.wait_ge(sem.xl, 16)
+        q.wait_ge(sem.xarr, nx)
+    for eng, a, b in PIECES:
+        src = T.win[:].indirect(T.offs[:, a // 16:b // 16])
+        if eng == "v":
+            done = vi(V.tensor_copy(T.ysb[:, a:b], src))
+            g.sync.wait_ge(sem.v, done)
+        else:
+            done = si(S.activation(T.ysb[:, a:b], src, F.Copy))
+            g.sync.wait_ge(sem.s, done)
+        g.sync.dma_start(T.y[:, a:b], T.ysb[:, a:b]).then_inc(sem.st, 16)
+
+    g.sync.wait_ge(sem.st, 16 * len(PIECES))
+    g.wait_ge(sem.lsent, ones_in(one))
+    g.wait_ge(sem.xsent, ones_in(wide))

@@ -5,46 +5,40 @@ R, J, Q, P = 4, 256, 2048, 128
 NJ = R * J
 K = NJ // P
 C = Q // 16
+H = C // 2
 SW = 144
-PIECES = [("v", 0, 384), ("s", 384, 768), ("v", 768, 1408), ("s", 1408, 2048)]
+IX = C + 5
+PIECES = [[(0, 128, 256), (256, 608, 1024)], [(1024, 1312, 1600), (1600, 1824, 2048)]]
 
 SCRATCH = {
     "win": ("sbuf", [P, NJ + 4], "float32"),
     "ysb": ("sbuf", [P, Q], "float32"),
-    "lall": ("dram", [R * P, J // P], "int32"),
     "lsb": ("sbuf", [P, K], "int32"),
     "lf": ("sbuf", [P, K], "float32"),
     "ones": ("sbuf", [P, K], "float32"),
     "scan": ("sbuf", [P, K + 4], "float32"),
-    "colk": ("sbuf", [P, P], "int32"),
-    "ck2": ("sbuf", [P, P], "int32"),
-    "rowp": ("sbuf", [P, 4], "int32"),
-    "t5": ("sbuf", [P, 4], "int32"),
-    "t1": ("sbuf", [P, 4], "int32"),
-    "th": ("sbuf", [P, 4], "int32"),
-    "tu": ("sbuf", [P, 4], "int32"),
-    "tv": ("sbuf", [P, 4], "int32"),
-    "key2": ("sbuf", [P, 4], "float32"),
-    "keyf": ("sbuf", [P, 4], "float32"),
-    "meq": ("sbuf", [P, P], "float32"),
+    "ix": ("sbuf", [P, IX], "int32"),
+    "i7": ("sbuf", [P, IX], "int32"),
+    "i3": ("sbuf", [P, IX], "int32"),
+    "iv": ("sbuf", [P, IX], "int32"),
+    "il": ("sbuf", [P, P], "int32"),
+    "key": ("sbuf", [P, IX], "float32"),
     "mle": ("sbuf", [P, P], "float32"),
-    "mlt": ("sbuf", [P, P], "float32"),
-    "meqp": ("sbuf", [P, P], "float32"),
-    "meqn": ("sbuf", [P, P], "float32"),
-    "nb": ("sbuf", [P, K], "float32"),
-    "cumi": ("sbuf", [P, K], "int32"),
-    "loi": ("sbuf", [P, K], "int32"),
-    "lof": ("sbuf", [P, K], "float32"),
-    "grid": ("sbuf", [P, C + 4], "float32"),
+    "mone": ("sbuf", [P, P], "float32"),
+    "rel": ("sbuf", [P, K], "float32"),
+    "hi": ("sbuf", [P, K], "int32"),
+    "lo": ("sbuf", [P, K], "bfloat16"),
+    "grid": ("sbuf", [P, C + 4], "bfloat16"),
     "ltab": ("sbuf", [P, P], "bfloat16"),
     "sg": ("sbuf", [P, K * SW], "bfloat16"),
     "gt": ("sbuf", [P, K * P], "bfloat16"),
     "le": ("sbuf", [P, K * P], "bfloat16"),
     "offs": ("sbuf", [P, C], "uint16"),
     "pcum": ("psum", [P, 512], "float32"),
-    "pcnt": ("psum", [P, 512], "float32"),
+    "pcnt0": ("psum", [P, 512], "float32"),
+    "pcnt1": ("psum", [P, 512], "float32"),
 }
-SEMAPHORES = ["lnl", "xl", "larr", "xarr", "lsent", "xsent", "lld", "gi", "v", "s", "t", "st"]
+SEMAPHORES = ["lnl", "xl", "larr", "xarr", "lsent", "xsent", "gi", "v", "s", "t", "st"]
 
 
 def ones_in(mask):
@@ -58,41 +52,36 @@ def rank_program(g, core, T, topo):
     A = AluOpType
     F = ActivationFunctionType
     sem = T.sem
+    V, S, E = g.vector, g.scalar, g.tensor
     n = len(T.cores)
     peers = [T.cores[(rank + i) % n] for i in range(1, n)]
     wide = topo.mask(core, peers[0])
     for d in peers:
         wide &= topo.mask(core, d)
-    one = wide & -wide
     dst = []
     for d in peers:
         rid, pnc = topo.addr(d, core)
         dst.append(DstId(rid=rid, pnc=pnc))
-    lslot = T.lall[rank * P:(rank + 1) * P, :]
+    lslot = T.lsb[:, 2 * rank:2 * rank + 2]
     xslot = T.win[:, rank * J:(rank + 1) * J]
-    SALL = (n - 1)
+    m = n - 1
+    w = ones_in(wide)
 
-    g.sync.dma_start(lslot, T.ln[:]).then_inc(sem.lnl, 16)
-    g.scalar.dma_start(xslot, T.x[:]).then_inc(sem.xl, 16)
+    g.sync.dma_start(T.lsb[:, 2 * rank:2 * rank + 1], T.ln[:, 0:8]).then_inc(sem.lnl, 16)
+    S.dma_start(T.lsb[:, 2 * rank + 1:2 * rank + 2], T.ln[:, 8:16]).then_inc(sem.lnl, 16)
+    g.sync.dma_start(xslot, T.x[:]).then_inc(sem.xl, 16)
 
-    g.iota(T.colk[:], [[32, 4], [1, 16], [16, 2]], 0, 0).then_inc(sem.gi, 1)
-    g.iota(T.rowp[:, 0:1], [[0, 1]], 0, 1).then_inc(sem.gi, 1)
-    g.wait_ge(sem.lnl, 16)
-    g.remote_dma_fused([RemoteDMATransfer(dst_ids=dst, dma_engine_mask=one, remote_sem=sem.larr,
-                                          srcs=[lslot], dsts=[lslot] * SALL)], local_sem=sem.lsent)
+    g.iota(T.ix[:, 0:C + 1], [[1, C + 1]], 0, 0).then_inc(sem.gi, 1)
+    g.iota(T.ix[:, C + 1:IX], [[0, IX - C - 1]], 0, 1).then_inc(sem.gi, 1)
+    g.wait_ge(sem.lnl, 32)
+    g.remote_dma_fused([RemoteDMATransfer(dst_ids=dst, dma_engine_mask=wide, remote_sem=sem.larr,
+                                          srcs=[lslot], dsts=[lslot] * m)], local_sem=sem.lsent)
     g.wait_ge(sem.xl, 16)
     g.remote_dma_fused([RemoteDMATransfer(dst_ids=dst, dma_engine_mask=wide, remote_sem=sem.xarr,
-                                          srcs=[xslot], dsts=[xslot] * SALL)], local_sem=sem.xsent)
-    g.iota(T.grid[:, 0:C + 1], [[32, C + 1]], 2 * rank * Q - 1, 0,
-           allow_small_or_imprecise_dtypes=True).then_inc(sem.gi, 1)
-    g.iota(T.ltab[:], [[0, P // 16], [1, 16]], 0, 0, allow_small_or_imprecise_dtypes=True).then_inc(sem.gi, 1)
-
-    g.sync.wait_ge(sem.lnl, 16)
-    g.sync.wait_ge(sem.larr, SALL * ones_in(one))
-    g.sync.dma_start(T.lsb[:], T.lall[:]).then_inc(sem.lld, 16)
+                                          srcs=[xslot], dsts=[xslot] * m)], local_sem=sem.xsent)
 
     vn = [0]
-    V = g.vector
+    sn = [0]
 
     def vi(ins):
         ins.then_inc(sem.v, 1)
@@ -102,94 +91,81 @@ def rank_program(g, core, T, topo):
     def vw():
         V.wait_ge(sem.v, vn[0])
 
-    vi(V.memset(T.win[:, NJ:NJ + 4], 0.0))
-    vi(V.memset(T.scan[:, 0:1], 0.0))
-    vi(V.memset(T.ones[:], 1.0))
-    V.wait_ge(sem.gi, 2)
-    vi(V.tensor_scalar(T.ck2[:], T.colk[:], 4, None, A.arith_shift_right))
-    vi(V.tensor_scalar(T.t5[:, 0:1], T.rowp[:, 0:1], 5, None, A.arith_shift_right))
-    vi(V.tensor_scalar(T.t1[:, 0:1], T.rowp[:, 0:1], 1, None, A.bitwise_and))
-    vi(V.tensor_scalar(T.th[:, 0:1], T.rowp[:, 0:1], 1, None, A.arith_shift_right))
-    vw()
-    vi(V.tensor_tensor(T.tu[:, 0:1], T.t5[:, 0:1], T.t1[:, 0:1], A.add))
-    vw()
-    vi(V.tensor_tensor(T.key2[:, 0:1], T.tu[:, 0:1], T.t5[:, 0:1], A.add))
-    vi(V.tensor_scalar(T.tv[:, 0:1], T.tu[:, 0:1], 16.0, None, A.mult))
-    vw()
-    vi(V.tensor_tensor(T.keyf[:, 0:1], T.tv[:, 0:1], T.th[:, 0:1], A.add))
-    vi(V.tensor_scalar(T.meq[:], T.ck2[:], T.key2[:, 0:1], None, A.is_equal))
-    vi(V.tensor_scalar(T.mlt[:], T.ck2[:], T.key2[:, 0:1], None, A.is_gt))
-    vw()
-    vi(V.tensor_scalar(T.mle[:], T.colk[:], T.keyf[:, 0:1], None, A.is_ge))
-    vw()
-    vi(V.tensor_tensor(T.meqp[:], T.meq[:], T.mle[:], A.mult))
-    vw()
-    vi(V.tensor_tensor(T.meqn[:], T.meq[:], T.meqp[:], A.subtract))
-
-    V.wait_ge(sem.lld, 16)
-    vi(V.tensor_copy(T.lf[:], T.lsb[:]))
-    vw()
-    v_scan = vi(V.tensor_tensor_scan(T.scan[:, 1:K + 1], T.ones[:], T.lf[:], 0.0, A.mult, A.add))
-
-    g.tensor.wait_ge(sem.v, v_scan)
-    g.tensor.matmul(T.pcum[:, K:K + 1], T.mlt[:], T.scan[:, K:K + 1], True, True)
-    g.tensor.matmul(T.pcum[:, 0:K], T.meqp[:], T.scan[:, 1:K + 1], True, False)
-    g.tensor.matmul(T.pcum[:, 0:K], T.meqn[:], T.scan[:, 0:K], False, True).then_inc(sem.t, 1)
-
-    V.wait_ge(sem.t, 1)
-    vi(V.tensor_scalar(T.cumi[:], T.pcum[:, 0:K], T.pcum[:, K:K + 1], None, A.add))
-    v_nb = vi(V.tensor_scalar(T.nb[:], T.pcum[:, 0:K], T.pcum[:, K:K + 1], -2.0, A.add, A.mult))
-    vw()
-    vi(V.tensor_scalar(T.loi[:], T.cumi[:], 15, None, A.bitwise_and))
-    vw()
-    vi(V.tensor_copy(T.lof[:], T.loi[:]))
-    vw()
-    V.wait_ge(sem.gi, 4)
-    v_cmp = []
-    for k in range(K):
-        vi(V.tensor_scalar(T.gt[:, k * P:(k + 1) * P], T.ltab[:], T.lof[:, k:k + 1], None, A.is_lt))
-        v_cmp.append(vi(V.tensor_scalar(T.le[:, k * P:(k + 1) * P], T.ltab[:], T.lof[:, k:k + 1], None, A.is_ge)))
-
-    sn = [0]
-    S = g.scalar
-
     def si(ins):
         ins.then_inc(sem.s, 1)
         sn[0] += 1
         return sn[0]
 
-    S.wait_ge(sem.gi, 4)
-    S.wait_ge(sem.v, v_nb)
+    vi(V.memset(T.scan[:, 0:1], 0.0))
+    vi(V.memset(T.ones[:], 1.0))
+    vi(V.memset(T.win[:, NJ:NJ + 4], 0.0))
+    vi(V.memset(T.mone[:], 0.0625))
+    V.wait_ge(sem.gi, 2)
+    vi(V.tensor_scalar(T.i7[:], T.ix[:], 7, None, A.bitwise_and))
+    vi(V.tensor_scalar(T.i3[:], T.ix[:], 3, None, A.arith_shift_right))
+    vi(V.tensor_scalar(T.il[:], T.ix[:, 0:P], 15, None, A.bitwise_and))
+    vw()
+    vi(V.tensor_scalar(T.iv[:], T.i7[:], 16.0, None, A.mult))
+    vw()
+    vi(V.tensor_tensor(T.key[:], T.iv[:], T.i3[:], A.add))
+    vw()
+    vi(V.tensor_scalar(T.mle[:], T.key[:, 0:P], T.key[:, C + 1:C + 2], 0.0625, A.is_ge, A.mult))
+    vi(V.tensor_scalar(T.ltab[:], T.il[:], 0.0625, 0.03125, A.mult, A.add))
+    vi(V.tensor_copy(T.grid[:, 0:C + 1], T.ix[:, 0:C + 1]))
+
+    V.wait_ge(sem.lnl, 32)
+    V.wait_ge(sem.larr, m * w)
+    v_lf = vi(V.tensor_copy(T.lf[:], T.lsb[:]))
+    vw()
+    v_scan = vi(V.tensor_tensor_scan(T.scan[:, 1:K + 1], T.ones[:], T.lf[:], 0.0, A.mult, A.add))
+
+    E.wait_ge(sem.v, v_lf)
+    E.matmul(T.pcum[:, 0:K], T.mle[:], T.lf[:], True, False)
+    E.wait_ge(sem.v, v_scan)
+    E.matmul(T.pcum[:, 0:K], T.mone[:], T.scan[:, 0:K], False, True).then_inc(sem.t, 1)
+
+    V.wait_ge(sem.t, 1)
+    v_rel = vi(V.tensor_scalar(T.rel[:], T.pcum[:, 0:K], 0.03125 - float(C * rank), None, A.add))
+    vi(V.tensor_scalar(T.hi[:], T.pcum[:, 0:K], -0.46875 - float(C * rank), None, A.add))
+    vw()
+    vi(V.tensor_tensor(T.lo[:], T.rel[:], T.hi[:], A.subtract))
+    vw()
+    v_cmp = []
+    for k in range(K):
+        vi(V.tensor_scalar(T.gt[:, k * P:(k + 1) * P], T.ltab[:], T.lo[:, k:k + 1], None, A.is_lt))
+        v_cmp.append(vi(V.tensor_scalar(T.le[:, k * P:(k + 1) * P], T.ltab[:], T.lo[:, k:k + 1], None, A.is_ge)))
+
+    S.wait_ge(sem.v, v_rel)
     s_sg = []
     for k in range(K):
         s_sg.append(si(S.activation(T.sg[:, k * SW:k * SW + C + 1], T.grid[:, 0:C + 1], F.Sign,
-                                    bias=T.nb[:, k:k + 1])))
+                                    bias=T.rel[:, k:k + 1], scale=-1.0)))
 
-    for k in range(K):
-        g.tensor.wait_ge(sem.v, v_cmp[k])
-        g.tensor.wait_ge(sem.s, s_sg[k])
-        g.tensor.matmul(T.pcnt[:, 0:C], T.gt[:, k * P:(k + 1) * P], T.sg[:, k * SW:k * SW + C], k == 0, False)
-        last = g.tensor.matmul(T.pcnt[:, 0:C], T.le[:, k * P:(k + 1) * P], T.sg[:, k * SW + 1:k * SW + C + 1],
-                               False, k == K - 1)
-    last.then_inc(sem.t, 1)
+    for h, out in enumerate((T.pcnt0, T.pcnt1)):
+        for k in range(K):
+            if h == 0:
+                E.wait_ge(sem.v, v_cmp[k])
+                E.wait_ge(sem.s, s_sg[k])
+            a = k * SW + h * H
+            E.matmul(out[:, 0:H], T.gt[:, k * P:(k + 1) * P], T.sg[:, a:a + H], k == 0, False)
+            last = E.matmul(out[:, 0:H], T.le[:, k * P:(k + 1) * P], T.sg[:, a + 1:a + H + 1], False, k == K - 1)
+        last.then_inc(sem.t, 1)
 
-    V.wait_ge(sem.t, 2)
-    v_off = vi(V.tensor_scalar(T.offs[:], T.pcnt[:, 0:C], 0.5, float(NJ // 2), A.mult, A.add))
-    nx = SALL * ones_in(wide)
-    for q in (V, S):
-        q.wait_ge(sem.v, v_off)
-        q.wait_ge(sem.xl, 16)
-        q.wait_ge(sem.xarr, nx)
-    for eng, a, b in PIECES:
-        src = T.win[:].indirect(T.offs[:, a // 16:b // 16])
-        if eng == "v":
-            done = vi(V.tensor_copy(T.ysb[:, a:b], src))
-            g.sync.wait_ge(sem.v, done)
-        else:
-            done = si(S.activation(T.ysb[:, a:b], src, F.Copy))
-            g.sync.wait_ge(sem.s, done)
-        g.sync.dma_start(T.y[:, a:b], T.ysb[:, a:b]).then_inc(sem.st, 16)
+    for h, cnt in enumerate((T.pcnt0, T.pcnt1)):
+        V.wait_ge(sem.t, 2 + h)
+        v_off = vi(V.tensor_scalar(T.offs[:, h * H:(h + 1) * H], cnt[:, 0:H], -0.5, float(NJ // 2), A.mult, A.add))
+        for q in (V, S):
+            q.wait_ge(sem.v, v_off)
+            if h == 0:
+                q.wait_ge(sem.xl, 16)
+                q.wait_ge(sem.xarr, m * w)
+        for a, b, c in PIECES[h]:
+            vd = vi(V.tensor_copy(T.ysb[:, a:b], T.win[:].indirect(T.offs[:, a // 16:b // 16])))
+            sd = si(S.activation(T.ysb[:, b:c], T.win[:].indirect(T.offs[:, b // 16:c // 16]), F.Copy))
+            g.sync.wait_ge(sem.v, vd)
+            g.sync.wait_ge(sem.s, sd)
+            g.sync.dma_start(T.y[:, a:c], T.ysb[:, a:c]).then_inc(sem.st, 16)
 
-    g.sync.wait_ge(sem.st, 16 * len(PIECES))
-    g.wait_ge(sem.lsent, ones_in(one))
-    g.wait_ge(sem.xsent, ones_in(wide))
+    g.sync.wait_ge(sem.st, 16 * (len(PIECES[0]) + len(PIECES[1])))
+    g.wait_ge(sem.lsent, w)
+    g.wait_ge(sem.xsent, w)

from concourse.bass import DstId, RemoteDMATransfer
from concourse.mybir import dt, AluOpType, ActivationFunctionType

R, J, Q, P = 4, 256, 2048, 128
NJ = R * J
K = NJ // P
C = Q // 16
H = C // 2
SW = 144
IX = C + 5
PIECES = [[(0, 128, 256), (256, 608, 1024)], [(1024, 1312, 1600), (1600, 1824, 2048)]]

SCRATCH = {
    "win": ("sbuf", [P, NJ + 4], "float32"),
    "ysb": ("sbuf", [P, Q], "float32"),
    "lsb": ("sbuf", [P, K], "int32"),
    "lf": ("sbuf", [P, K], "float32"),
    "ones": ("sbuf", [P, K], "float32"),
    "scan": ("sbuf", [P, K + 4], "float32"),
    "ix": ("sbuf", [P, IX], "int32"),
    "i7": ("sbuf", [P, IX], "int32"),
    "i3": ("sbuf", [P, IX], "int32"),
    "iv": ("sbuf", [P, IX], "int32"),
    "il": ("sbuf", [P, P], "int32"),
    "key": ("sbuf", [P, IX], "float32"),
    "mle": ("sbuf", [P, P], "float32"),
    "mone": ("sbuf", [P, P], "float32"),
    "rel": ("sbuf", [P, K], "float32"),
    "hi": ("sbuf", [P, K], "int32"),
    "lo": ("sbuf", [P, K], "bfloat16"),
    "grid": ("sbuf", [P, C + 4], "bfloat16"),
    "ltab": ("sbuf", [P, P], "bfloat16"),
    "sg": ("sbuf", [P, K * SW], "bfloat16"),
    "gt": ("sbuf", [P, K * P], "bfloat16"),
    "le": ("sbuf", [P, K * P], "bfloat16"),
    "offs": ("sbuf", [P, C], "uint16"),
    "pcum": ("psum", [P, 512], "float32"),
    "pcnt0": ("psum", [P, 512], "float32"),
    "pcnt1": ("psum", [P, 512], "float32"),
}
SEMAPHORES = ["lnl", "xl", "larr", "xarr", "lsent", "xsent", "gi", "v", "s", "t", "st"]


def ones_in(mask):
    return bin(mask).count("1")


def rank_program(g, core, T, topo):
    rank = T.rank_of(core)
    if rank is None:
        return
    A = AluOpType
    F = ActivationFunctionType
    sem = T.sem
    V, S, E = g.vector, g.scalar, g.tensor
    n = len(T.cores)
    peers = [T.cores[(rank + i) % n] for i in range(1, n)]
    wide = topo.mask(core, peers[0])
    for d in peers:
        wide &= topo.mask(core, d)
    dst = []
    for d in peers:
        rid, pnc = topo.addr(d, core)
        dst.append(DstId(rid=rid, pnc=pnc))
    lslot = T.lsb[:, 2 * rank:2 * rank + 2]
    xslot = T.win[:, rank * J:(rank + 1) * J]
    m = n - 1
    w = ones_in(wide)

    g.sync.dma_start(T.lsb[:, 2 * rank:2 * rank + 1], T.ln[:, 0:8]).then_inc(sem.lnl, 16)
    S.dma_start(T.lsb[:, 2 * rank + 1:2 * rank + 2], T.ln[:, 8:16]).then_inc(sem.lnl, 16)
    g.sync.dma_start(xslot, T.x[:]).then_inc(sem.xl, 16)

    g.iota(T.ix[:, 0:C + 1], [[1, C + 1]], 0, 0).then_inc(sem.gi, 1)
    g.iota(T.ix[:, C + 1:IX], [[0, IX - C - 1]], 0, 1).then_inc(sem.gi, 1)
    g.wait_ge(sem.lnl, 32)
    g.remote_dma_fused([RemoteDMATransfer(dst_ids=dst, dma_engine_mask=wide, remote_sem=sem.larr,
                                          srcs=[lslot], dsts=[lslot] * m)], local_sem=sem.lsent)
    g.wait_ge(sem.xl, 16)
    g.remote_dma_fused([RemoteDMATransfer(dst_ids=dst, dma_engine_mask=wide, remote_sem=sem.xarr,
                                          srcs=[xslot], dsts=[xslot] * m)], local_sem=sem.xsent)

    vn = [0]
    sn = [0]

    def vi(ins):
        ins.then_inc(sem.v, 1)
        vn[0] += 1
        return vn[0]

    def vw():
        V.wait_ge(sem.v, vn[0])

    def si(ins):
        ins.then_inc(sem.s, 1)
        sn[0] += 1
        return sn[0]

    vi(V.memset(T.scan[:, 0:1], 0.0))
    vi(V.memset(T.ones[:], 1.0))
    vi(V.memset(T.win[:, NJ:NJ + 4], 0.0))
    vi(V.memset(T.mone[:], 0.0625))
    V.wait_ge(sem.gi, 2)
    vi(V.tensor_scalar(T.i7[:], T.ix[:], 7, None, A.bitwise_and))
    vi(V.tensor_scalar(T.i3[:], T.ix[:], 3, None, A.arith_shift_right))
    vi(V.tensor_scalar(T.il[:], T.ix[:, 0:P], 15, None, A.bitwise_and))
    vw()
    vi(V.tensor_scalar(T.iv[:], T.i7[:], 16.0, None, A.mult))
    vw()
    vi(V.tensor_tensor(T.key[:], T.iv[:], T.i3[:], A.add))
    vw()
    vi(V.tensor_scalar(T.mle[:], T.key[:, 0:P], T.key[:, C + 1:C + 2], 0.0625, A.is_ge, A.mult))
    vi(V.tensor_scalar(T.ltab[:], T.il[:], 0.0625, 0.03125, A.mult, A.add))
    vi(V.tensor_copy(T.grid[:, 0:C + 1], T.ix[:, 0:C + 1]))

    V.wait_ge(sem.lnl, 32)
    V.wait_ge(sem.larr, m * w)
    v_lf = vi(V.tensor_copy(T.lf[:], T.lsb[:]))
    vw()
    v_scan = vi(V.tensor_tensor_scan(T.scan[:, 1:K + 1], T.ones[:], T.lf[:], 0.0, A.mult, A.add))

    E.wait_ge(sem.v, v_lf)
    E.matmul(T.pcum[:, 0:K], T.mle[:], T.lf[:], True, False)
    E.wait_ge(sem.v, v_scan)
    E.matmul(T.pcum[:, 0:K], T.mone[:], T.scan[:, 0:K], False, True).then_inc(sem.t, 1)

    V.wait_ge(sem.t, 1)
    v_rel = vi(V.tensor_scalar(T.rel[:], T.pcum[:, 0:K], 0.03125 - float(C * rank), None, A.add))
    vi(V.tensor_scalar(T.hi[:], T.pcum[:, 0:K], -0.46875 - float(C * rank), None, A.add))
    vw()
    vi(V.tensor_tensor(T.lo[:], T.rel[:], T.hi[:], A.subtract))
    vw()
    v_cmp = []
    for k in range(K):
        vi(V.tensor_scalar(T.gt[:, k * P:(k + 1) * P], T.ltab[:], T.lo[:, k:k + 1], None, A.is_lt))
        v_cmp.append(vi(V.tensor_scalar(T.le[:, k * P:(k + 1) * P], T.ltab[:], T.lo[:, k:k + 1], None, A.is_ge)))

    S.wait_ge(sem.v, v_rel)
    s_sg = []
    for k in range(K):
        s_sg.append(si(S.activation(T.sg[:, k * SW:k * SW + C + 1], T.grid[:, 0:C + 1], F.Sign,
                                    bias=T.rel[:, k:k + 1], scale=-1.0)))

    for h, out in enumerate((T.pcnt0, T.pcnt1)):
        for k in range(K):
            if h == 0:
                E.wait_ge(sem.v, v_cmp[k])
                E.wait_ge(sem.s, s_sg[k])
            a = k * SW + h * H
            E.matmul(out[:, 0:H], T.gt[:, k * P:(k + 1) * P], T.sg[:, a:a + H], k == 0, False)
            last = E.matmul(out[:, 0:H], T.le[:, k * P:(k + 1) * P], T.sg[:, a + 1:a + H + 1], False, k == K - 1)
        last.then_inc(sem.t, 1)

    for h, cnt in enumerate((T.pcnt0, T.pcnt1)):
        V.wait_ge(sem.t, 2 + h)
        v_off = vi(V.tensor_scalar(T.offs[:, h * H:(h + 1) * H], cnt[:, 0:H], -0.5, float(NJ // 2), A.mult, A.add))
        for q in (V, S):
            q.wait_ge(sem.v, v_off)
            if h == 0:
                q.wait_ge(sem.xl, 16)
                q.wait_ge(sem.xarr, m * w)
        for a, b, c in PIECES[h]:
            vd = vi(V.tensor_copy(T.ysb[:, a:b], T.win[:].indirect(T.offs[:, a // 16:b // 16])))
            sd = si(S.activation(T.ysb[:, b:c], T.win[:].indirect(T.offs[:, b // 16:c // 16]), F.Copy))
            g.sync.wait_ge(sem.v, vd)
            g.sync.wait_ge(sem.s, sd)
            g.sync.dma_start(T.y[:, a:c], T.ysb[:, a:c]).then_inc(sem.st, 16)

    g.sync.wait_ge(sem.st, 16 * (len(PIECES[0]) + len(PIECES[1])))
    g.wait_ge(sem.lsent, w)
    g.wait_ge(sem.xsent, w)
